import numpy as np
import ml_dtypes


def mxq(x, axis, fmt="e4m3"):
    dtype, down = {"e4m3": (ml_dtypes.float8_e4m3fn, 7), "e5m2": (ml_dtypes.float8_e5m2, 14)}[fmt]
    v = np.moveaxis(np.asarray(x, np.float32).astype(ml_dtypes.bfloat16).astype(np.float64), axis, -1)
    blocks = v.reshape(v.shape[:-1] + (-1, 32))
    amax = np.abs(blocks).max(-1, keepdims=True)
    byte = np.maximum(np.where(amax > 0, np.frexp(amax)[1] - 1 + 127, 0) - down, 1)
    scale = np.exp2(byte - 127.0)
    codes = (blocks / scale).astype(np.float32).astype(dtype).astype(np.float64)
    return np.moveaxis((codes * scale).reshape(v.shape), -1, axis)


WIDE = False


def mx_kscale(k):
    if not WIDE:
        return np.ones(k)
    levels = np.array([30, -30])
    if k % 512:
        return np.exp2(np.random.permutation(np.resize(levels, k // 32))).repeat(32)
    a = np.empty((k // 512, 16))
    for p in range(k // 512):
        a[p, :8] = np.random.permutation(np.resize(levels, 8))
        for g in range(8):
            far = levels[np.abs(levels - a[p, g]) >= 10]
            a[p, g + 8] = far[np.random.randint(len(far))]
    return np.exp2(a.ravel()).repeat(32)


def f64(x):
    return np.asarray(x).astype(np.float64)


def striped(idx):
    return np.tile(np.asarray(idx).reshape(-1, 16).T, (8, 1)).astype(np.uint16)


def unstriped(offs):
    return offs[:16].T.reshape(-1).astype(np.int64)


E2M1 = np.array([0.0, 0.5, 1.0, 1.5, 2.0, 3.0, 4.0, 6.0, -0.0, -0.5, -1.0, -1.5, -2.0, -3.0, -4.0, -6.0])


def pack_weight(w, fmt):
    k, n = w.shape
    w = f64(np.asarray(w, np.float32).astype(ml_dtypes.bfloat16)).reshape(k // 32, 32, n)
    amax = np.abs(w).max(1)
    if fmt in ("e4m3", "e5m2"):
        byte = np.frexp(amax)[1] - 1 + 127 - (7 if fmt == "e4m3" else 14)
    else:
        mant, ex = np.frexp(amax / 6.0)
        byte = np.where(mant > 0.5, ex, ex - 1) + 127
    byte = np.clip(np.where(amax > 0, byte, 1), 1, 254)
    scaled = (w * np.exp2(127.0 - byte)[:, None, :]).reshape(k, n).astype(np.float32)
    by_word = np.ascontiguousarray(scaled.reshape(k // 512, 128, 4, n).transpose(0, 1, 3, 2))
    if fmt in ("e4m3", "e5m2"):
        words = by_word.astype(ml_dtypes.float8_e4m3fn if fmt == "e4m3" else ml_dtypes.float8_e5m2).view(np.uint8)
    else:
        c = by_word.astype(ml_dtypes.float4_e2m1fn).view(np.uint8) & 0xF
        words = (c[..., 0::2] | (c[..., 1::2] << 4)).reshape(k // 512, 128, 2 * n)
    return np.ascontiguousarray(words), np.ascontiguousarray(byte.astype(np.uint8).reshape(k // 512, 16, n))


def unpack_weight(words, scales, fmt):
    g, _, n = scales.shape
    words = np.ascontiguousarray(words).reshape(g, 128, n, -1)
    if fmt in ("e4m3", "e5m2"):
        vals = words.view(ml_dtypes.float8_e4m3fn if fmt == "e4m3" else ml_dtypes.float8_e5m2).astype(np.float64)
    else:
        nib = np.empty((g, 128, n, 4), np.uint8)
        nib[..., 0::2] = words & 0xF
        nib[..., 1::2] = words >> 4
        vals = E2M1[nib]
    vals = vals * np.repeat(np.exp2(scales.astype(np.float64) - 127.0), 8, axis=1)[..., None]
    return vals.transpose(0, 1, 3, 2).reshape(g * 512, n)


K, T, J, B, R, O, N, C = 512, 512, 256, 32, 512, 128, 256, 1024


def setup_inputs():
    n = np.random.standard_normal
    idx = np.random.permutation(T)[:J]
    idx2 = np.random.permutation(J)[:O]
    idx3 = np.random.permutation(J)[:O]
    idx4 = np.random.permutation(C)[:O]
    fk = mx_kscale(K)
    fr = mx_kscale(R)
    wp = pack_weight(n((K, R)) * 1 / np.sqrt(K) * fk[:, None] * fr, "e2m1")
    wbp = pack_weight(n((R, N)) * 1 / np.sqrt(R) / fr[:, None], "e5m2")
    return {
        "xf": (n((K, T))).astype(np.float32),
        "fk": (np.random.uniform(0.5, 2.0, (K, 1)) / fk[:, None]).astype(np.float32),
        "w_words": wp[0],
        "w_scales": wp[1],
        "wb_words": wbp[0],
        "wb_scales": wbp[1],
        "old": (1.0 * n((N, C))).astype(np.float32),
        "offs": striped(idx),
        "offs2": striped(idx2),
        "offs3": striped(idx3),
        "offs4": striped(idx4),
    }


def reference(xf, fk, w_words, w_scales, wb_words, wb_scales, old, offs, offs2, offs3, offs4):
    idx = unstriped(offs)
    idx2 = unstriped(offs2)
    idx3 = unstriped(offs3)
    idx4 = unstriped(offs4)
    wu = unpack_weight(w_words, w_scales, "e2m1")
    wbu = unpack_weight(wb_words, wb_scales, "e5m2")
    xg = f64(xf)[:, idx]
    g1 = xg.reshape(K, B, J // B).mean(axis=2)
    g2 = np.repeat(g1, J // B, axis=1)
    u = (xg - g2) * f64(fk)
    uq = mxq(u, 0, "e4m3")
    a = wu.T @ uq
    hid = np.abs(a[:, idx2] - 0.5 * a[:, idx3])
    hidq = mxq(hid, 0, "e5m2")
    p = wbu.T @ hidq
    pp = np.zeros((N, C))
    pp[:, idx4] = p
    y = pp + 0.5 * f64(old)
    return y

@@ -1,0 +1,225 @@
+from contextlib import ExitStack
+
+import concourse.mybir as mybir
+
+K, T, J, R, O, N, C = 512, 512, 256, 512, 128, 256, 1024
+GROUP = 8
+B = J // GROUP
+P = 128
+PACK = 4
+FLOPS = 2 * K * R * J + 2 * R * N * O
+
+F32 = mybir.dt.float32
+BF16 = mybir.dt.bfloat16
+I32 = mybir.dt.int32
+U32 = mybir.dt.uint32
+U16 = mybir.dt.uint16
+U8 = mybir.dt.uint8
+E4M3 = mybir.dt.float8_e4m3fn_x4
+E5M2 = mybir.dt.float8_e5m2_x4
+E2M1 = mybir.dt.float4_e2m1fn_x4
+ALU = mybir.AluOpType
+ACT = mybir.ActivationFunctionType
+AXIS = mybir.AxisListType
+CHUNK = 512
+
+
+def tile_list_looks_centredpicks_farther_scattered_kernel(
+    tc, xf, fk, w_words, w_scales, wb_words, wb_scales, old, offs, offs2, offs3, offs4, out
+):
+    nc = tc.nc
+    with ExitStack() as ctx:
+        lists = ctx.enter_context(tc.tile_pool(name="lists", bufs=1))
+        sb = ctx.enter_context(tc.tile_pool(name="sb", bufs=1))
+        psum = ctx.enter_context(tc.psum_pool(name="psum", bufs=1))
+
+        idx = lists.tile([P, J // 16], U16, name="idx")
+        idx2 = lists.tile([P, O // 16], U16, name="idx2")
+        idx3 = lists.tile([P, O // 16], U16, name="idx3")
+        idx4 = lists.tile([P, O // 16], U16, name="idx4")
+
+        ws_raw = sb.tile([P, R], U8, name="ws_raw", align_bytes=64)
+        wb_s = sb.tile([P, N], U8, name="wb_s", align_bytes=64)
+        nc.gpsimd.memset(ws_raw[:].bitcast(U32), 0)
+        nc.vector.memset(wb_s[:].bitcast(U32), 0)
+
+        x_rows = xf.rearrange("(p i) t -> p i t", i=PACK)
+        x = [sb.tile([P, T], F32, name=f"x{i}") for i in range(PACK)]
+        fk_sb = sb.tile([P, PACK], F32, name="fk_sb")
+        w_raw = sb.tile([P, 2 * R], U8, name="w_raw", align_bytes=64)
+        wb_w = sb.tile([P, N], U32, name="wb_w", align_bytes=64)
+        old_sb = [sb.tile([P, C], F32, name=f"old{h}") for h in range(N // P)]
+
+        nc.sync.dma_start(idx[:], offs)
+        nc.gpsimd.dma_start(fk_sb[:], fk.rearrange("(p i) o -> p (i o)", i=PACK))
+        for i in range(PACK - 1):
+            nc.sync.dma_start(x[i][:], x_rows[:, i, :])
+        for q in range(4):
+            nc.scalar.dma_start(ws_raw[32 * q : 32 * q + 4, :].bitcast(I32), w_scales[0, 4 * q : 4 * q + 4, :].bitcast(I32))
+        warm_in = sb.tile([P, 1], F32, name="warm_in")
+        warm_out = sb.tile([P, 1], F32, name="warm_out")
+        nc.gpsimd.memset(warm_in[:], 0.0)
+        nc.scalar.activation(warm_out[:], warm_in[:], ACT.Abs)
+        nc.sync.dma_start(x[PACK - 1][:], x_rows[:, PACK - 1, :])
+        nc.sync.dma_start(w_raw[:].bitcast(I32), w_words[0].bitcast(I32))
+        nc.sync.dma_start(idx3[:], offs3)
+        nc.sync.dma_start(idx2[:], offs2)
+        nc.sync.dma_start(wb_w[:].bitcast(I32), wb_words[0].rearrange("p n r -> p (n r)").bitcast(I32))
+        for q in range(4):
+            nc.sync.dma_start(wb_s[32 * q : 32 * q + 4, :].bitcast(I32), wb_scales[0, 4 * q : 4 * q + 4, :].bitcast(I32))
+        nc.sync.dma_start(idx4[:], offs4)
+        for h in range(N // P):
+            nc.sync.dma_start(old_sb[h][:], old[h * P : (h + 1) * P, :])
+
+        page = [sb.tile([P, C], F32, name=f"page{h}") for h in range(N // P)]
+        for h in range(N // P):
+            nc.vector.memset(page[h][:], 0.0)
+
+        xg = [sb.tile([P, J], F32, name=f"xg{i}") for i in range(PACK)]
+        sums = [sb.tile([P, B], F32, name=f"sums{i}") for i in range(PACK)]
+        shift = [sb.tile([P, B], F32, name=f"shift{i}") for i in range(PACK)]
+        u_pair = [sb.tile([P, 2, J], F32, name=f"u_pair{e}") for e in range(2)]
+        u_bf = sb.tile([P, J, PACK], BF16, name="u_bf", align_bytes=64)
+        u_w = sb.tile([P, J], U32, name="u_w", align_bytes=64)
+        u_s = sb.tile([P, J], U8, name="u_s", align_bytes=64)
+
+        w_dealt = sb.tile([P, 2 * R], U8, name="w_dealt", align_bytes=64)
+        ws_dealt = sb.tile([P, R], U8, name="ws_dealt", align_bytes=64)
+        nc.vector.tensor_copy(
+            ws_dealt[:].rearrange("p (t m) -> p t m", t=PACK), ws_raw[:].rearrange("p (m t) -> p t m", t=PACK)
+        )
+
+        whole = (0, J)
+        halves = ((0, J // 2), (J // 2, J))
+
+        def grouped(ap, j0, j1):
+            return ap[:, j0:j1].rearrange("p (b m) -> p b m", m=GROUP)
+
+        def pick_scalar(i, j0, j1):
+            nc.scalar.activation(xg[i][:, j0:j1], x[i][:].indirect(idx[:, j0 // 16 : j1 // 16]), ACT.Copy)
+
+        def group_sums(i, j0, j1):
+            nc.vector.tensor_reduce(sums[i][:, j0 // GROUP : j1 // GROUP], grouped(xg[i], j0, j1), AXIS.X, ALU.add)
+
+        def scaled_mean(i, j0, j1):
+            b0, b1 = j0 // GROUP, j1 // GROUP
+            nc.vector.tensor_scalar(
+                shift[i][:, b0:b1], sums[i][:, b0:b1], fk_sb[:, i : i + 1], 1.0 / GROUP, ALU.mult, ALU.mult
+            )
+
+        def centre(i, j0, j1):
+            b0, b1 = j0 // GROUP, j1 // GROUP
+            nc.vector.scalar_tensor_tensor(
+                grouped(u_pair[i // 2][:, i % 2, :], j0, j1),
+                grouped(xg[i], j0, j1),
+                fk_sb[:, i : i + 1],
+                shift[i][:, b0:b1].unsqueeze(2).to_broadcast([P, b1 - b0, GROUP]),
+                ALU.mult,
+                ALU.subtract,
+            )
+
+        def weave_upper(j0, j1):
+            nc.vector.tensor_copy(u_bf[:, j0:j1, 2:4], u_pair[1][:, :, j0:j1].rearrange("p e j -> p j e"))
+
+        def quantise_u(j0, j1):
+            nc.vector.quantize_mx(
+                out=u_w[:, j0:j1].bitcast(E4M3), scales=u_s[:, j0:j1], in_=u_bf[:, j0:j1, :].rearrange("p j i -> p (j i)")
+            )
+
+        last = PACK - 1
+        pick_scalar(0, *halves[0])
+        nc.vector.tensor_copy(xg[0][:, J // 2 :], x[0][:].indirect(idx[:, J // 32 :]))
+        group_sums(0, *whole)
+        scaled_mean(0, *whole)
+        for i in range(1, last):
+            pick_scalar(i, *whole)
+            group_sums(i, *whole)
+            centre(i - 1, *whole)
+            scaled_mean(i, *whole)
+        for half_j in halves:
+            pick_scalar(last, *half_j)
+        group_sums(last, *halves[0])
+        centre(last - 1, *whole)
+        group_sums(last, *halves[1])
+        nc.scalar.copy(u_bf[:, :, 0:2], u_pair[0][:].rearrange("p e j -> p j e"))
+        for half_j in halves:
+            scaled_mean(last, *half_j)
+        for half_j in halves:
+            centre(last, *half_j)
+        for half_j in halves:
+            weave_upper(*half_j)
+        for half_j in halves:
+            quantise_u(*half_j)
+
+        nc.scalar.copy(
+            w_dealt[:].bitcast(U16).rearrange("p (t m) -> p t m", t=PACK),
+            w_raw[:].bitcast(U16).rearrange("p (m t) -> p t m", t=PACK),
+        )
+
+        a_ps = [psum.tile([P, J], F32, name=f"a_ps{t}") for t in range(PACK)]
+        a = [sb.tile([P, J], F32, name=f"a{t}") for t in range(PACK)]
+        half = [sb.tile([P, O], F32, name=f"half{t}") for t in range(PACK)]
+        diff = sb.tile([P, PACK, O], F32, name="diff")
+        for t in range(PACK):
+            nc.tensor.matmul_mx(
+                out=a_ps[t][:],
+                lhsT=w_dealt[:, 2 * P * t : 2 * P * (t + 1)].bitcast(E2M1),
+                lhsT_scale=ws_dealt[:, P * t : P * (t + 1)],
+                rhs=u_w[:].bitcast(E4M3),
+                rhs_scale=u_s[:],
+                start=True,
+                stop=True,
+            )
+
+        def look3(t):
+            nc.scalar.activation(half[t][:], a[t][:].indirect(idx3[:]), ACT.Copy, scale=-0.5)
+
+        def look2(t):
+            nc.vector.tensor_tensor(diff[:, t, :], a[t][:].indirect(idx2[:]), half[t][:], ALU.add)
+
+        nc.scalar.copy(a[0][:], a_ps[0][:])
+        nc.vector.tensor_copy(a[1][:], a_ps[1][:])
+        look3(0)
+        nc.vector.tensor_copy(a[2][:], a_ps[2][:])
+        look3(1)
+        look2(0)
+        nc.scalar.copy(a[3][:], a_ps[3][:])
+        look2(1)
+        for t in range(2, PACK):
+            look3(t)
+            look2(t)
+
+        hid_bf = sb.tile([P, O, PACK], BF16, name="hid_bf", align_bytes=64)
+        hid_w = sb.tile([P, O], U32, name="hid_w", align_bytes=64)
+        hid_s = sb.tile([P, O], U8, name="hid_s", align_bytes=64)
+        woven = diff[:].rearrange("p t o -> p o t")
+        nc.scalar.activation(hid_bf[:, : O // 2, :], woven[:, : O // 2, :], ACT.Abs)
+        nc.vector.scalar_tensor_tensor(
+            hid_bf[:, O // 2 :, :], woven[:, O // 2 :, :], -1.0, woven[:, O // 2 :, :], ALU.mult, ALU.max
+        )
+        nc.vector.quantize_mx(out=hid_w[:].bitcast(E5M2), scales=hid_s[:], in_=hid_bf[:].rearrange("p o t -> p (o t)"))
+
+        p_ps = [psum.tile([P, O], F32, name=f"p_ps{h}") for h in range(N // P)]
+        p_sb = [sb.tile([P, O], F32, name=f"p_sb{h}") for h in range(N // P)]
+        for h in range(N // P):
+            nc.tensor.matmul_mx(
+                out=p_ps[h][:],
+                lhsT=wb_w[:, P * h : P * (h + 1)].bitcast(E5M2),
+                lhsT_scale=wb_s[:, P * h : P * (h + 1)],
+                rhs=hid_w[:].bitcast(E5M2),
+                rhs_scale=hid_s[:],
+                start=True,
+                stop=True,
+            )
+        nc.vector.tensor_copy(p_sb[0][:], p_ps[0][:])
+        nc.scalar.copy(p_sb[1][:], p_ps[1][:])
+        nc.vector.tensor_copy(page[0][:].indirect(idx4[:]), p_sb[0][:])
+        nc.scalar.activation(page[1][:].indirect(idx4[:]), p_sb[1][:], ACT.Copy)
+
+        for h in range(N // P):
+            for c0 in range(0, C, CHUNK):
+                y = sb.tile([P, CHUNK], F32, name=f"y{h}_{c0}")
+                nc.vector.scalar_tensor_tensor(
+                    y[:], old_sb[h][:, c0 : c0 + CHUNK], 0.5, page[h][:, c0 : c0 + CHUNK], ALU.mult, ALU.add
+                )
+                nc.sync.dma_start(out[h * P : (h + 1) * P, c0 : c0 + CHUNK], y[:])

@@ -40,54 +40,43 @@ def tile_list_looks_centredpicks_farther_scattered_kernel(
 
         ws_raw = sb.tile([P, R], U8, name="ws_raw", align_bytes=64)
         wb_s = sb.tile([P, N], U8, name="wb_s", align_bytes=64)
-        nc.gpsimd.memset(ws_raw[:].bitcast(U32), 0)
-        nc.vector.memset(wb_s[:].bitcast(U32), 0)
-
-        x_rows = xf.rearrange("(p i) t -> p i t", i=PACK)
-        x = [sb.tile([P, T], F32, name=f"x{i}") for i in range(PACK)]
-        fk_sb = sb.tile([P, PACK], F32, name="fk_sb")
-        w_raw = sb.tile([P, 2 * R], U8, name="w_raw", align_bytes=64)
-        wb_w = sb.tile([P, N], U32, name="wb_w", align_bytes=64)
-        old_sb = [sb.tile([P, C], F32, name=f"old{h}") for h in range(N // P)]
-
-        nc.sync.dma_start(idx[:], offs)
-        nc.gpsimd.dma_start(fk_sb[:], fk.rearrange("(p i) o -> p (i o)", i=PACK))
-        for i in range(PACK - 1):
-            nc.sync.dma_start(x[i][:], x_rows[:, i, :])
-        for q in range(4):
-            nc.scalar.dma_start(ws_raw[32 * q : 32 * q + 4, :].bitcast(I32), w_scales[0, 4 * q : 4 * q + 4, :].bitcast(I32))
         warm_in = sb.tile([P, 1], F32, name="warm_in")
         warm_out = sb.tile([P, 1], F32, name="warm_out")
         nc.gpsimd.memset(warm_in[:], 0.0)
+        nc.gpsimd.memset(ws_raw[:].bitcast(U32), 0)
+        nc.gpsimd.memset(wb_s[:].bitcast(U32), 0)
+
+        x_rows = xf.rearrange("(p i) t -> p i t", i=PACK)
+        x = [sb.tile([P, T], F32, name=f"x{i}", tag=f"rows{i}", align_bytes=64) for i in range(PACK)]
+        fk_sb = sb.tile([P, PACK], F32, name="fk_sb")
+        w_raw = sb.tile([P, 2 * R], U8, name="w_raw", align_bytes=64)
+        wb_w = sb.tile([P, N], U32, name="wb_w", align_bytes=64)
+
+        nc.scalar.dma_start(fk_sb[:], fk.rearrange("(p i) o -> p (i o)", i=PACK))
         nc.scalar.activation(warm_out[:], warm_in[:], ACT.Abs)
-        nc.sync.dma_start(x[PACK - 1][:], x_rows[:, PACK - 1, :])
+        nc.sync.dma_start(idx[:], offs)
+        for i in range(PACK):
+            nc.sync.dma_start(x[i][:], x_rows[:, i, :])
         nc.sync.dma_start(w_raw[:].bitcast(I32), w_words[0].bitcast(I32))
+        for q in range(4):
+            nc.sync.dma_start(ws_raw[32 * q : 32 * q + 4, :].bitcast(I32), w_scales[0, 4 * q : 4 * q + 4, :].bitcast(I32))
         nc.sync.dma_start(idx3[:], offs3)
         nc.sync.dma_start(idx2[:], offs2)
         nc.sync.dma_start(wb_w[:].bitcast(I32), wb_words[0].rearrange("p n r -> p (n r)").bitcast(I32))
         for q in range(4):
             nc.sync.dma_start(wb_s[32 * q : 32 * q + 4, :].bitcast(I32), wb_scales[0, 4 * q : 4 * q + 4, :].bitcast(I32))
         nc.sync.dma_start(idx4[:], offs4)
-        for h in range(N // P):
-            nc.sync.dma_start(old_sb[h][:], old[h * P : (h + 1) * P, :])
 
         page = [sb.tile([P, C], F32, name=f"page{h}") for h in range(N // P)]
         for h in range(N // P):
             nc.vector.memset(page[h][:], 0.0)
 
         xg = [sb.tile([P, J], F32, name=f"xg{i}") for i in range(PACK)]
-        sums = [sb.tile([P, B], F32, name=f"sums{i}") for i in range(PACK)]
-        shift = [sb.tile([P, B], F32, name=f"shift{i}") for i in range(PACK)]
-        u_pair = [sb.tile([P, 2, J], F32, name=f"u_pair{e}") for e in range(2)]
-        u_bf = sb.tile([P, J, PACK], BF16, name="u_bf", align_bytes=64)
+        sums = [sb.tile([P, B], F32, name=f"sums{i}", tag=f"sums{i}", align_bytes=64) for i in range(PACK)]
+        cen = [sb.tile([P, J], F32, name=f"cen{i}", tag=f"cen{i}", align_bytes=64) for i in range(PACK)]
+        u_bf = sb.tile([P, J, PACK], BF16, name="u_bf", tag=f"rows{PACK - 1}", align_bytes=64)
         u_w = sb.tile([P, J], U32, name="u_w", align_bytes=64)
         u_s = sb.tile([P, J], U8, name="u_s", align_bytes=64)
-
-        w_dealt = sb.tile([P, 2 * R], U8, name="w_dealt", align_bytes=64)
-        ws_dealt = sb.tile([P, R], U8, name="ws_dealt", align_bytes=64)
-        nc.vector.tensor_copy(
-            ws_dealt[:].rearrange("p (t m) -> p t m", t=PACK), ws_raw[:].rearrange("p (m t) -> p t m", t=PACK)
-        )
 
         whole = (0, J)
         halves = ((0, J // 2), (J // 2, J))
@@ -101,25 +90,19 @@ def tile_list_looks_centredpicks_farther_scattered_kernel(
         def group_sums(i, j0, j1):
             nc.vector.tensor_reduce(sums[i][:, j0 // GROUP : j1 // GROUP], grouped(xg[i], j0, j1), AXIS.X, ALU.add)
 
-        def scaled_mean(i, j0, j1):
-            b0, b1 = j0 // GROUP, j1 // GROUP
-            nc.vector.tensor_scalar(
-                shift[i][:, b0:b1], sums[i][:, b0:b1], fk_sb[:, i : i + 1], 1.0 / GROUP, ALU.mult, ALU.mult
-            )
-
         def centre(i, j0, j1):
             b0, b1 = j0 // GROUP, j1 // GROUP
             nc.vector.scalar_tensor_tensor(
-                grouped(u_pair[i // 2][:, i % 2, :], j0, j1),
+                grouped(cen[i], j0, j1),
+                sums[i][:, b0:b1].unsqueeze(2).to_broadcast([P, b1 - b0, GROUP]),
+                -1.0 / GROUP,
                 grouped(xg[i], j0, j1),
-                fk_sb[:, i : i + 1],
-                shift[i][:, b0:b1].unsqueeze(2).to_broadcast([P, b1 - b0, GROUP]),
                 ALU.mult,
-                ALU.subtract,
+                ALU.add,
             )
 
-        def weave_upper(j0, j1):
-            nc.vector.tensor_copy(u_bf[:, j0:j1, 2:4], u_pair[1][:, :, j0:j1].rearrange("p e j -> p j e"))
+        def scale_vector(i, j0, j1):
+            nc.vector.tensor_scalar(u_bf[:, j0:j1, i], cen[i][:, j0:j1], fk_sb[:, i : i + 1], None, ALU.mult)
 
         def quantise_u(j0, j1):
             nc.vector.quantize_mx(
@@ -129,32 +112,40 @@ def tile_list_looks_centredpicks_farther_scattered_kernel(
         last = PACK - 1
         pick_scalar(0, *halves[0])
         nc.vector.tensor_copy(xg[0][:, J // 2 :], x[0][:].indirect(idx[:, J // 32 :]))
-        group_sums(0, *whole)
-        scaled_mean(0, *whole)
-        for i in range(1, last):
-            pick_scalar(i, *whole)
+        for i in range(last):
+            if i > 0:
+                pick_scalar(i, *whole)
             group_sums(i, *whole)
-            centre(i - 1, *whole)
-            scaled_mean(i, *whole)
+            if i < last - 1:
+                centre(i, *whole)
         for half_j in halves:
             pick_scalar(last, *half_j)
+        for i in range(2):
+            nc.scalar.activation(u_bf[:, :, i], cen[i][:], ACT.Copy, scale=fk_sb[:, i : i + 1])
         group_sums(last, *halves[0])
         centre(last - 1, *whole)
         group_sums(last, *halves[1])
-        nc.scalar.copy(u_bf[:, :, 0:2], u_pair[0][:].rearrange("p e j -> p j e"))
+        centre(last, *halves[0])
+        scale_vector(last - 1, *whole)
+        centre(last, *halves[1])
         for half_j in halves:
-            scaled_mean(last, *half_j)
-        for half_j in halves:
-            centre(last, *half_j)
-        for half_j in halves:
-            weave_upper(*half_j)
+            scale_vector(last, *half_j)
         for half_j in halves:
             quantise_u(*half_j)
 
-        nc.scalar.copy(
-            w_dealt[:].bitcast(U16).rearrange("p (t m) -> p t m", t=PACK),
-            w_raw[:].bitcast(U16).rearrange("p (m t) -> p t m", t=PACK),
-        )
+        w_by_t = w_raw[:].bitcast(U16).rearrange("p (m t) -> p t m", t=PACK)
+        w_dealt = sb.tile([P, PACK * 2 * P], U8, name="w_dealt", tag="cen0", align_bytes=64)
+        for t in range(PACK):
+            nc.scalar.copy(w_dealt[:, 2 * P * t : 2 * P * (t + 1)].bitcast(U16), w_by_t[:, t, :])
+        ws_by_t = ws_raw[:].rearrange("p (m t) -> p t m", t=PACK)
+        ws_first = sb.tile([P, P], U8, name="ws_first", tag=f"sums{last - 1}", align_bytes=64)
+        ws_rest = sb.tile([P, last, P], U8, name="ws_rest", tag=f"cen{last}", align_bytes=64)
+        nc.vector.tensor_copy(ws_first[:], ws_by_t[:, 0, :])
+        nc.vector.tensor_copy(ws_rest[:], ws_by_t[:, 1:, :])
+        ws_dealt = [ws_first[:]] + [ws_rest[:, t, :] for t in range(last)]
+        old_sb = [sb.tile([P, C], F32, name=f"old{h}", tag=f"rows{h + 2}", align_bytes=64) for h in range(N // P)]
+        for h in range(N // P):
+            nc.sync.dma_start(old_sb[h][:], old[h * P : (h + 1) * P, :])
 
         a_ps = [psum.tile([P, J], F32, name=f"a_ps{t}") for t in range(PACK)]
         a = [sb.tile([P, J], F32, name=f"a{t}") for t in range(PACK)]
@@ -164,7 +155,7 @@ def tile_list_looks_centredpicks_farther_scattered_kernel(
             nc.tensor.matmul_mx(
                 out=a_ps[t][:],
                 lhsT=w_dealt[:, 2 * P * t : 2 * P * (t + 1)].bitcast(E2M1),
-                lhsT_scale=ws_dealt[:, P * t : P * (t + 1)],
+                lhsT_scale=ws_dealt[t],
                 rhs=u_w[:].bitcast(E4M3),
                 rhs_scale=u_s[:],
                 start=True,
@@ -177,15 +168,11 @@ def tile_list_looks_centredpicks_farther_scattered_kernel(
         def look2(t):
             nc.vector.tensor_tensor(diff[:, t, :], a[t][:].indirect(idx2[:]), half[t][:], ALU.add)
 
-        nc.scalar.copy(a[0][:], a_ps[0][:])
-        nc.vector.tensor_copy(a[1][:], a_ps[1][:])
-        look3(0)
-        nc.vector.tensor_copy(a[2][:], a_ps[2][:])
-        look3(1)
-        look2(0)
-        nc.scalar.copy(a[3][:], a_ps[3][:])
-        look2(1)
+        for t in range(2):
+            nc.scalar.copy(a[t][:], a_ps[t][:])
         for t in range(2, PACK):
+            nc.vector.tensor_copy(a[t][:], a_ps[t][:])
+        for t in range(PACK):
             look3(t)
             look2(t)
 

@@ -7,6 +7,10 @@ GROUP = 8
 B = J // GROUP
 P = 128
 PACK = 4
+LIST_ROWS = 16
+QUADRANTS, QUADRANT = 4, 32
+PAGES = N // P
+CHUNK = 256
 FLOPS = 2 * K * R * J + 2 * R * N * O
 
 F32 = mybir.dt.float32
@@ -21,7 +25,13 @@ E2M1 = mybir.dt.float4_e2m1fn_x4
 ALU = mybir.AluOpType
 ACT = mybir.ActivationFunctionType
 AXIS = mybir.AxisListType
-CHUNK = 512
+
+
+def load_scale_rows(nc, tile, scales):
+    for q in range(QUADRANTS):
+        nc.sync.dma_start(
+            tile[QUADRANT * q : QUADRANT * q + 4, :].bitcast(I32), scales[0, 4 * q : 4 * q + 4, :].bitcast(I32)
+        )
 
 
 def tile_list_looks_centredpicks_farther_scattered_kernel(
@@ -33,17 +43,17 @@ def tile_list_looks_centredpicks_farther_scattered_kernel(
         sb = ctx.enter_context(tc.tile_pool(name="sb", bufs=1))
         psum = ctx.enter_context(tc.psum_pool(name="psum", bufs=1))
 
-        idx = lists.tile([P, J // 16], U16, name="idx")
-        idx2 = lists.tile([P, O // 16], U16, name="idx2")
-        idx3 = lists.tile([P, O // 16], U16, name="idx3")
-        idx4 = lists.tile([P, O // 16], U16, name="idx4")
+        idx = lists.tile([P, J // LIST_ROWS], U16, name="idx")
+        idx2 = lists.tile([P, O // LIST_ROWS], U16, name="idx2")
+        idx3 = lists.tile([P, O // LIST_ROWS], U16, name="idx3")
+        idx4 = lists.tile([P, O // LIST_ROWS], U16, name="idx4")
 
         ws_raw = sb.tile([P, R], U8, name="ws_raw", align_bytes=64)
         wb_s = sb.tile([P, N], U8, name="wb_s", align_bytes=64)
         warm_in = sb.tile([P, 1], F32, name="warm_in")
         warm_out = sb.tile([P, 1], F32, name="warm_out")
-        nc.gpsimd.memset(warm_in[:], 0.0)
         nc.gpsimd.memset(ws_raw[:].bitcast(U32), 0)
+        nc.gpsimd.memset(warm_in[:], 0.0)
         nc.gpsimd.memset(wb_s[:].bitcast(U32), 0)
 
         x_rows = xf.rearrange("(p i) t -> p i t", i=PACK)
@@ -52,129 +62,151 @@ def tile_list_looks_centredpicks_farther_scattered_kernel(
         w_raw = sb.tile([P, 2 * R], U8, name="w_raw", align_bytes=64)
         wb_w = sb.tile([P, N], U32, name="wb_w", align_bytes=64)
 
-        nc.scalar.dma_start(fk_sb[:], fk.rearrange("(p i) o -> p (i o)", i=PACK))
         nc.scalar.activation(warm_out[:], warm_in[:], ACT.Abs)
+
         nc.sync.dma_start(idx[:], offs)
-        for i in range(PACK):
+        nc.sync.dma_start(x[0][:], x_rows[:, 0, :])
+        load_scale_rows(nc, ws_raw, w_scales)
+        for i in range(1, PACK):
             nc.sync.dma_start(x[i][:], x_rows[:, i, :])
+        nc.sync.dma_start(fk_sb[:], fk.rearrange("(p i) o -> p (i o)", i=PACK))
         nc.sync.dma_start(w_raw[:].bitcast(I32), w_words[0].bitcast(I32))
-        for q in range(4):
-            nc.sync.dma_start(ws_raw[32 * q : 32 * q + 4, :].bitcast(I32), w_scales[0, 4 * q : 4 * q + 4, :].bitcast(I32))
         nc.sync.dma_start(idx3[:], offs3)
         nc.sync.dma_start(idx2[:], offs2)
         nc.sync.dma_start(wb_w[:].bitcast(I32), wb_words[0].rearrange("p n r -> p (n r)").bitcast(I32))
-        for q in range(4):
-            nc.sync.dma_start(wb_s[32 * q : 32 * q + 4, :].bitcast(I32), wb_scales[0, 4 * q : 4 * q + 4, :].bitcast(I32))
+        load_scale_rows(nc, wb_s, wb_scales)
         nc.sync.dma_start(idx4[:], offs4)
 
-        page = [sb.tile([P, C], F32, name=f"page{h}") for h in range(N // P)]
-        for h in range(N // P):
+        page = [sb.tile([P, C], F32, name=f"page{h}") for h in range(PAGES)]
+        for h in range(PAGES):
             nc.vector.memset(page[h][:], 0.0)
 
         xg = [sb.tile([P, J], F32, name=f"xg{i}") for i in range(PACK)]
-        sums = [sb.tile([P, B], F32, name=f"sums{i}", tag=f"sums{i}", align_bytes=64) for i in range(PACK)]
-        cen = [sb.tile([P, J], F32, name=f"cen{i}", tag=f"cen{i}", align_bytes=64) for i in range(PACK)]
-        u_bf = sb.tile([P, J, PACK], BF16, name="u_bf", tag=f"rows{PACK - 1}", align_bytes=64)
+        sums = [sb.tile([P, B], F32, name=f"sums{i}") for i in range(PACK)]
+        centred0 = sb.tile([P, J], F32, name="centred0")
+        shift = [sb.tile([P, B], F32, name=f"shift{e}", align_bytes=64) for e in range(2)]
+        u_upper = sb.tile([P, 2, J], F32, name="u_upper", align_bytes=64)
+        u_lower = sb.tile([P, 2, J], F32, name="u_lower", tag="u_lower", align_bytes=64)
+        u_bf = sb.tile([P, J, PACK], BF16, name="u_bf", align_bytes=64)
         u_w = sb.tile([P, J], U32, name="u_w", align_bytes=64)
         u_s = sb.tile([P, J], U8, name="u_s", align_bytes=64)
 
         whole = (0, J)
         halves = ((0, J // 2), (J // 2, J))
 
-        def grouped(ap, j0, j1):
-            return ap[:, j0:j1].rearrange("p (b m) -> p b m", m=GROUP)
+        def grouped(tile, j0, j1):
+            return tile[:, j0:j1].rearrange("p (b m) -> p b m", m=GROUP)
 
-        def pick_scalar(i, j0, j1):
-            nc.scalar.activation(xg[i][:, j0:j1], x[i][:].indirect(idx[:, j0 // 16 : j1 // 16]), ACT.Copy)
+        def spread(tile, j0, j1):
+            b0, b1 = j0 // GROUP, j1 // GROUP
+            return tile[:, b0:b1].unsqueeze(2).to_broadcast([P, b1 - b0, GROUP])
+
+        def listed(i, j0, j1):
+            return x[i][:].indirect(idx[:, j0 // LIST_ROWS : j1 // LIST_ROWS])
+
+        def pick_on_scalar(i, j0, j1):
+            nc.scalar.activation(xg[i][:, j0:j1], listed(i, j0, j1), ACT.Copy)
 
         def group_sums(i, j0, j1):
             nc.vector.tensor_reduce(sums[i][:, j0 // GROUP : j1 // GROUP], grouped(xg[i], j0, j1), AXIS.X, ALU.add)
 
-        def centre(i, j0, j1):
-            b0, b1 = j0 // GROUP, j1 // GROUP
+        def centre(i, centred):
             nc.vector.scalar_tensor_tensor(
-                grouped(cen[i], j0, j1),
-                sums[i][:, b0:b1].unsqueeze(2).to_broadcast([P, b1 - b0, GROUP]),
-                -1.0 / GROUP,
-                grouped(xg[i], j0, j1),
-                ALU.mult,
-                ALU.add,
+                grouped(centred, *whole), spread(sums[i], *whole), -1.0 / GROUP, grouped(xg[i], *whole), ALU.mult, ALU.add
             )
 
-        def scale_vector(i, j0, j1):
-            nc.vector.tensor_scalar(u_bf[:, j0:j1, i], cen[i][:, j0:j1], fk_sb[:, i : i + 1], None, ALU.mult)
+        def scaled_mean(i, j0, j1):
+            b0, b1 = j0 // GROUP, j1 // GROUP
+            nc.vector.tensor_scalar(
+                shift[i - 2][:, b0:b1], sums[i][:, b0:b1], fk_sb[:, i : i + 1], 1.0 / GROUP, ALU.mult, ALU.mult
+            )
 
-        def quantise_u(j0, j1):
+        def centre_scaled(i, j0, j1):
+            nc.vector.scalar_tensor_tensor(
+                grouped(u_upper[:, i - 2, :], j0, j1),
+                grouped(xg[i], j0, j1),
+                fk_sb[:, i : i + 1],
+                spread(shift[i - 2], j0, j1),
+                ALU.mult,
+                ALU.subtract,
+            )
+
+        pick_on_scalar(0, *halves[0])
+        nc.vector.tensor_copy(xg[0][:, J // 2 :], listed(0, *halves[1]))
+        pick_on_scalar(1, *whole)
+        pick_on_scalar(2, *whole)
+        for j0, j1 in halves:
+            pick_on_scalar(3, j0, j1)
+        centred1 = sb.tile([P, J], F32, name="centred1", tag="rows2", align_bytes=64)
+        group_sums(0, *whole)
+        centre(0, centred0)
+        group_sums(1, *whole)
+        group_sums(2, *whole)
+        centre(1, centred1)
+        for i, centred in enumerate((centred0, centred1)):
+            nc.scalar.activation(u_lower[:, i, :], centred[:], ACT.Copy, scale=fk_sb[:, i : i + 1])
+        for j0, j1 in halves:
+            nc.scalar.copy(u_bf[:, j0:j1, 0:2], u_lower[:, :, j0:j1].rearrange("p e j -> p j e"))
+        scaled_mean(2, *whole)
+        for j0, j1 in halves:
+            group_sums(3, j0, j1)
+        scaled_mean(3, *halves[0])
+        centre_scaled(2, *whole)
+        scaled_mean(3, *halves[1])
+        for j0, j1 in halves:
+            centre_scaled(3, j0, j1)
+        for j0, j1 in halves:
+            nc.vector.tensor_copy(u_bf[:, j0:j1, 2:4], u_upper[:, :, j0:j1].rearrange("p e j -> p j e"))
+        for j0, j1 in halves:
             nc.vector.quantize_mx(
                 out=u_w[:, j0:j1].bitcast(E4M3), scales=u_s[:, j0:j1], in_=u_bf[:, j0:j1, :].rearrange("p j i -> p (j i)")
             )
 
-        last = PACK - 1
-        pick_scalar(0, *halves[0])
-        nc.vector.tensor_copy(xg[0][:, J // 2 :], x[0][:].indirect(idx[:, J // 32 :]))
-        for i in range(last):
-            if i > 0:
-                pick_scalar(i, *whole)
-            group_sums(i, *whole)
-            if i < last - 1:
-                centre(i, *whole)
-        for half_j in halves:
-            pick_scalar(last, *half_j)
-        for i in range(2):
-            nc.scalar.activation(u_bf[:, :, i], cen[i][:], ACT.Copy, scale=fk_sb[:, i : i + 1])
-        group_sums(last, *halves[0])
-        centre(last - 1, *whole)
-        group_sums(last, *halves[1])
-        centre(last, *halves[0])
-        scale_vector(last - 1, *whole)
-        centre(last, *halves[1])
-        for half_j in halves:
-            scale_vector(last, *half_j)
-        for half_j in halves:
-            quantise_u(*half_j)
-
-        w_by_t = w_raw[:].bitcast(U16).rearrange("p (m t) -> p t m", t=PACK)
-        w_dealt = sb.tile([P, PACK * 2 * P], U8, name="w_dealt", tag="cen0", align_bytes=64)
-        for t in range(PACK):
-            nc.scalar.copy(w_dealt[:, 2 * P * t : 2 * P * (t + 1)].bitcast(U16), w_by_t[:, t, :])
-        ws_by_t = ws_raw[:].rearrange("p (m t) -> p t m", t=PACK)
-        ws_first = sb.tile([P, P], U8, name="ws_first", tag=f"sums{last - 1}", align_bytes=64)
-        ws_rest = sb.tile([P, last, P], U8, name="ws_rest", tag=f"cen{last}", align_bytes=64)
-        nc.vector.tensor_copy(ws_first[:], ws_by_t[:, 0, :])
-        nc.vector.tensor_copy(ws_rest[:], ws_by_t[:, 1:, :])
-        ws_dealt = [ws_first[:]] + [ws_rest[:, t, :] for t in range(last)]
-        old_sb = [sb.tile([P, C], F32, name=f"old{h}", tag=f"rows{h + 2}", align_bytes=64) for h in range(N // P)]
-        for h in range(N // P):
+        w_dealt = [
+            sb.tile([P, 2, 2 * P], U8, name="w_dealt0", align_bytes=64),
+            sb.tile([P, 2, 2 * P], U8, name="w_dealt1", tag="u_lower", align_bytes=64),
+        ]
+        w_by_plane = w_raw[:].bitcast(U16).rearrange("p (m t) -> p t m", t=PACK)
+        for e in range(2):
+            nc.scalar.copy(w_dealt[e][:].bitcast(U16), w_by_plane[:, 2 * e : 2 * e + 2, :])
+        ws_dealt = sb.tile([P, R], U8, name="ws_dealt", tag="rows0", align_bytes=64)
+        nc.vector.tensor_copy(
+            ws_dealt[:].rearrange("p (t m) -> p t m", t=PACK), ws_raw[:].rearrange("p (m t) -> p t m", t=PACK)
+        )
+        old_sb = [sb.tile([P, C], F32, name=f"old{h}", tag=f"rows{h + 2}", align_bytes=64) for h in range(PAGES)]
+        for h in range(PAGES):
             nc.sync.dma_start(old_sb[h][:], old[h * P : (h + 1) * P, :])
 
-        a_ps = [psum.tile([P, J], F32, name=f"a_ps{t}") for t in range(PACK)]
         a = [sb.tile([P, J], F32, name=f"a{t}") for t in range(PACK)]
-        half = [sb.tile([P, O], F32, name=f"half{t}") for t in range(PACK)]
+        minus_half = [sb.tile([P, O], F32, name=f"minus_half{t}") for t in range(PACK)]
         diff = sb.tile([P, PACK, O], F32, name="diff")
-        for t in range(PACK):
+
+        def first_product(t, j0, j1):
+            bank = psum.tile([P, j1 - j0], F32, name=f"a_ps{t}_{j0}")
             nc.tensor.matmul_mx(
-                out=a_ps[t][:],
-                lhsT=w_dealt[:, 2 * P * t : 2 * P * (t + 1)].bitcast(E2M1),
-                lhsT_scale=ws_dealt[t],
-                rhs=u_w[:].bitcast(E4M3),
-                rhs_scale=u_s[:],
+                out=bank[:],
+                lhsT=w_dealt[t // 2][:, t % 2, :].bitcast(E2M1),
+                lhsT_scale=ws_dealt[:, P * t : P * (t + 1)],
+                rhs=u_w[:, j0:j1].bitcast(E4M3),
+                rhs_scale=u_s[:, j0:j1],
                 start=True,
                 stop=True,
             )
+            return bank
 
-        def look3(t):
-            nc.scalar.activation(half[t][:], a[t][:].indirect(idx3[:]), ACT.Copy, scale=-0.5)
+        nc.scalar.copy(a[0][:, : J // 2], first_product(0, *halves[0])[:])
+        nc.vector.tensor_copy(a[0][:, J // 2 :], first_product(0, *halves[1])[:])
+        for t in range(1, PACK):
+            nc.vector.tensor_copy(a[t][:], first_product(t, *whole)[:])
 
-        def look2(t):
-            nc.vector.tensor_tensor(diff[:, t, :], a[t][:].indirect(idx2[:]), half[t][:], ALU.add)
-
-        for t in range(2):
-            nc.scalar.copy(a[t][:], a_ps[t][:])
-        for t in range(2, PACK):
-            nc.vector.tensor_copy(a[t][:], a_ps[t][:])
+        last = PACK - 1
         for t in range(PACK):
-            look3(t)
-            look2(t)
+            nc.scalar.activation(minus_half[t][:], a[t][:].indirect(idx3[:]), ACT.Copy, scale=-0.5)
+            if t < last:
+                nc.vector.tensor_tensor(diff[:, t, :], a[t][:].indirect(idx2[:]), minus_half[t][:], ALU.add)
+        looked_up = sb.tile([P, O], F32, name="looked_up")
+        nc.scalar.activation(looked_up[:], a[last][:].indirect(idx2[:]), ACT.Copy)
+        nc.vector.tensor_tensor(diff[:, last, :], looked_up[:], minus_half[last][:], ALU.add)
 
         hid_bf = sb.tile([P, O, PACK], BF16, name="hid_bf", align_bytes=64)
         hid_w = sb.tile([P, O], U32, name="hid_w", align_bytes=64)
@@ -186,9 +218,9 @@ def tile_list_looks_centredpicks_farther_scattered_kernel(
         )
         nc.vector.quantize_mx(out=hid_w[:].bitcast(E5M2), scales=hid_s[:], in_=hid_bf[:].rearrange("p o t -> p (o t)"))
 
-        p_ps = [psum.tile([P, O], F32, name=f"p_ps{h}") for h in range(N // P)]
-        p_sb = [sb.tile([P, O], F32, name=f"p_sb{h}") for h in range(N // P)]
-        for h in range(N // P):
+        p_ps = [psum.tile([P, O], F32, name=f"p_ps{h}") for h in range(PAGES)]
+        p_sb = [sb.tile([P, O], F32, name=f"p_sb{h}") for h in range(PAGES)]
+        for h in range(PAGES):
             nc.tensor.matmul_mx(
                 out=p_ps[h][:],
                 lhsT=wb_w[:, P * h : P * (h + 1)].bitcast(E5M2),
@@ -203,7 +235,7 @@ def tile_list_looks_centredpicks_farther_scattered_kernel(
         nc.vector.tensor_copy(page[0][:].indirect(idx4[:]), p_sb[0][:])
         nc.scalar.activation(page[1][:].indirect(idx4[:]), p_sb[1][:], ACT.Copy)
 
-        for h in range(N // P):
+        for h in range(PAGES):
             for c0 in range(0, C, CHUNK):
                 y = sb.tile([P, CHUNK], F32, name=f"y{h}_{c0}")
                 nc.vector.scalar_tensor_tensor(

from contextlib import ExitStack

import concourse.mybir as mybir

K, T, J, R, O, N, C = 512, 512, 256, 512, 128, 256, 1024
GROUP = 8
B = J // GROUP
P = 128
PACK = 4
LIST_ROWS = 16
QUADRANTS, QUADRANT = 4, 32
PAGES = N // P
CHUNK = 256
FLOPS = 2 * K * R * J + 2 * R * N * O

F32 = mybir.dt.float32
BF16 = mybir.dt.bfloat16
I32 = mybir.dt.int32
U32 = mybir.dt.uint32
U16 = mybir.dt.uint16
U8 = mybir.dt.uint8
E4M3 = mybir.dt.float8_e4m3fn_x4
E5M2 = mybir.dt.float8_e5m2_x4
E2M1 = mybir.dt.float4_e2m1fn_x4
ALU = mybir.AluOpType
ACT = mybir.ActivationFunctionType
AXIS = mybir.AxisListType


def load_scale_rows(nc, tile, scales):
    for q in range(QUADRANTS):
        nc.sync.dma_start(
            tile[QUADRANT * q : QUADRANT * q + 4, :].bitcast(I32), scales[0, 4 * q : 4 * q + 4, :].bitcast(I32)
        )


def tile_list_looks_centredpicks_farther_scattered_kernel(
    tc, xf, fk, w_words, w_scales, wb_words, wb_scales, old, offs, offs2, offs3, offs4, out
):
    nc = tc.nc
    with ExitStack() as ctx:
        lists = ctx.enter_context(tc.tile_pool(name="lists", bufs=1))
        sb = ctx.enter_context(tc.tile_pool(name="sb", bufs=1))
        psum = ctx.enter_context(tc.psum_pool(name="psum", bufs=1))

        idx = lists.tile([P, J // LIST_ROWS], U16, name="idx")
        idx2 = lists.tile([P, O // LIST_ROWS], U16, name="idx2")
        idx3 = lists.tile([P, O // LIST_ROWS], U16, name="idx3")
        idx4 = lists.tile([P, O // LIST_ROWS], U16, name="idx4")

        ws_raw = sb.tile([P, R], U8, name="ws_raw", align_bytes=64)
        wb_s = sb.tile([P, N], U8, name="wb_s", align_bytes=64)
        warm_in = sb.tile([P, 1], F32, name="warm_in")
        warm_out = sb.tile([P, 1], F32, name="warm_out")
        nc.gpsimd.memset(ws_raw[:].bitcast(U32), 0)
        nc.gpsimd.memset(warm_in[:], 0.0)
        nc.gpsimd.memset(wb_s[:].bitcast(U32), 0)

        x_rows = xf.rearrange("(p i) t -> p i t", i=PACK)
        x = [sb.tile([P, T], F32, name=f"x{i}", tag=f"rows{i}", align_bytes=64) for i in range(PACK)]
        fk_sb = sb.tile([P, PACK], F32, name="fk_sb")
        w_raw = sb.tile([P, 2 * R], U8, name="w_raw", align_bytes=64)
        wb_w = sb.tile([P, N], U32, name="wb_w", align_bytes=64)

        nc.scalar.activation(warm_out[:], warm_in[:], ACT.Abs)

        nc.sync.dma_start(idx[:], offs)
        nc.sync.dma_start(x[0][:], x_rows[:, 0, :])
        load_scale_rows(nc, ws_raw, w_scales)
        for i in range(1, PACK):
            nc.sync.dma_start(x[i][:], x_rows[:, i, :])
        nc.sync.dma_start(fk_sb[:], fk.rearrange("(p i) o -> p (i o)", i=PACK))
        nc.sync.dma_start(w_raw[:].bitcast(I32), w_words[0].bitcast(I32))
        nc.sync.dma_start(idx3[:], offs3)
        nc.sync.dma_start(idx2[:], offs2)
        nc.sync.dma_start(wb_w[:].bitcast(I32), wb_words[0].rearrange("p n r -> p (n r)").bitcast(I32))
        load_scale_rows(nc, wb_s, wb_scales)
        nc.sync.dma_start(idx4[:], offs4)

        page = [sb.tile([P, C], F32, name=f"page{h}") for h in range(PAGES)]
        for h in range(PAGES):
            nc.vector.memset(page[h][:], 0.0)

        xg = [sb.tile([P, J], F32, name=f"xg{i}") for i in range(PACK)]
        sums = [sb.tile([P, B], F32, name=f"sums{i}") for i in range(PACK)]
        centred0 = sb.tile([P, J], F32, name="centred0")
        shift = [sb.tile([P, B], F32, name=f"shift{e}", align_bytes=64) for e in range(2)]
        u_upper = sb.tile([P, 2, J], F32, name="u_upper", align_bytes=64)
        u_lower = sb.tile([P, 2, J], F32, name="u_lower", tag="u_lower", align_bytes=64)
        u_bf = sb.tile([P, J, PACK], BF16, name="u_bf", align_bytes=64)
        u_w = sb.tile([P, J], U32, name="u_w", align_bytes=64)
        u_s = sb.tile([P, J], U8, name="u_s", align_bytes=64)

        whole = (0, J)
        halves = ((0, J // 2), (J // 2, J))

        def grouped(tile, j0, j1):
            return tile[:, j0:j1].rearrange("p (b m) -> p b m", m=GROUP)

        def spread(tile, j0, j1):
            b0, b1 = j0 // GROUP, j1 // GROUP
            return tile[:, b0:b1].unsqueeze(2).to_broadcast([P, b1 - b0, GROUP])

        def listed(i, j0, j1):
            return x[i][:].indirect(idx[:, j0 // LIST_ROWS : j1 // LIST_ROWS])

        def pick_on_scalar(i, j0, j1):
            nc.scalar.activation(xg[i][:, j0:j1], listed(i, j0, j1), ACT.Copy)

        def group_sums(i, j0, j1):
            nc.vector.tensor_reduce(sums[i][:, j0 // GROUP : j1 // GROUP], grouped(xg[i], j0, j1), AXIS.X, ALU.add)

        def centre(i, centred):
            nc.vector.scalar_tensor_tensor(
                grouped(centred, *whole), spread(sums[i], *whole), -1.0 / GROUP, grouped(xg[i], *whole), ALU.mult, ALU.add
            )

        def scaled_mean(i, j0, j1):
            b0, b1 = j0 // GROUP, j1 // GROUP
            nc.vector.tensor_scalar(
                shift[i - 2][:, b0:b1], sums[i][:, b0:b1], fk_sb[:, i : i + 1], 1.0 / GROUP, ALU.mult, ALU.mult
            )

        def centre_scaled(i, j0, j1):
            nc.vector.scalar_tensor_tensor(
                grouped(u_upper[:, i - 2, :], j0, j1),
                grouped(xg[i], j0, j1),
                fk_sb[:, i : i + 1],
                spread(shift[i - 2], j0, j1),
                ALU.mult,
                ALU.subtract,
            )

        pick_on_scalar(0, *halves[0])
        nc.vector.tensor_copy(xg[0][:, J // 2 :], listed(0, *halves[1]))
        pick_on_scalar(1, *whole)
        pick_on_scalar(2, *whole)
        for j0, j1 in halves:
            pick_on_scalar(3, j0, j1)
        centred1 = sb.tile([P, J], F32, name="centred1", tag="rows2", align_bytes=64)
        group_sums(0, *whole)
        centre(0, centred0)
        group_sums(1, *whole)
        group_sums(2, *whole)
        centre(1, centred1)
        for i, centred in enumerate((centred0, centred1)):
            nc.scalar.activation(u_lower[:, i, :], centred[:], ACT.Copy, scale=fk_sb[:, i : i + 1])
        for j0, j1 in halves:
            nc.scalar.copy(u_bf[:, j0:j1, 0:2], u_lower[:, :, j0:j1].rearrange("p e j -> p j e"))
        scaled_mean(2, *whole)
        for j0, j1 in halves:
            group_sums(3, j0, j1)
        scaled_mean(3, *halves[0])
        centre_scaled(2, *whole)
        scaled_mean(3, *halves[1])
        for j0, j1 in halves:
            centre_scaled(3, j0, j1)
        for j0, j1 in halves:
            nc.vector.tensor_copy(u_bf[:, j0:j1, 2:4], u_upper[:, :, j0:j1].rearrange("p e j -> p j e"))
        for j0, j1 in halves:
            nc.vector.quantize_mx(
                out=u_w[:, j0:j1].bitcast(E4M3), scales=u_s[:, j0:j1], in_=u_bf[:, j0:j1, :].rearrange("p j i -> p (j i)")
            )

        w_dealt = [
            sb.tile([P, 2, 2 * P], U8, name="w_dealt0", align_bytes=64),
            sb.tile([P, 2, 2 * P], U8, name="w_dealt1", tag="u_lower", align_bytes=64),
        ]
        w_by_plane = w_raw[:].bitcast(U16).rearrange("p (m t) -> p t m", t=PACK)
        for e in range(2):
            nc.scalar.copy(w_dealt[e][:].bitcast(U16), w_by_plane[:, 2 * e : 2 * e + 2, :])
        ws_dealt = sb.tile([P, R], U8, name="ws_dealt", tag="rows0", align_bytes=64)
        nc.vector.tensor_copy(
            ws_dealt[:].rearrange("p (t m) -> p t m", t=PACK), ws_raw[:].rearrange("p (m t) -> p t m", t=PACK)
        )
        old_sb = [sb.tile([P, C], F32, name=f"old{h}", tag=f"rows{h + 2}", align_bytes=64) for h in range(PAGES)]
        for h in range(PAGES):
            nc.sync.dma_start(old_sb[h][:], old[h * P : (h + 1) * P, :])

        a = [sb.tile([P, J], F32, name=f"a{t}") for t in range(PACK)]
        minus_half = [sb.tile([P, O], F32, name=f"minus_half{t}") for t in range(PACK)]
        diff = sb.tile([P, PACK, O], F32, name="diff")

        def first_product(t, j0, j1):
            bank = psum.tile([P, j1 - j0], F32, name=f"a_ps{t}_{j0}")
            nc.tensor.matmul_mx(
                out=bank[:],
                lhsT=w_dealt[t // 2][:, t % 2, :].bitcast(E2M1),
                lhsT_scale=ws_dealt[:, P * t : P * (t + 1)],
                rhs=u_w[:, j0:j1].bitcast(E4M3),
                rhs_scale=u_s[:, j0:j1],
                start=True,
                stop=True,
            )
            return bank

        nc.scalar.copy(a[0][:, : J // 2], first_product(0, *halves[0])[:])
        nc.vector.tensor_copy(a[0][:, J // 2 :], first_product(0, *halves[1])[:])
        for t in range(1, PACK):
            nc.vector.tensor_copy(a[t][:], first_product(t, *whole)[:])

        last = PACK - 1
        for t in range(PACK):
            nc.scalar.activation(minus_half[t][:], a[t][:].indirect(idx3[:]), ACT.Copy, scale=-0.5)
            if t < last:
                nc.vector.tensor_tensor(diff[:, t, :], a[t][:].indirect(idx2[:]), minus_half[t][:], ALU.add)
        looked_up = sb.tile([P, O], F32, name="looked_up")
        nc.scalar.activation(looked_up[:], a[last][:].indirect(idx2[:]), ACT.Copy)
        nc.vector.tensor_tensor(diff[:, last, :], looked_up[:], minus_half[last][:], ALU.add)

        hid_bf = sb.tile([P, O, PACK], BF16, name="hid_bf", align_bytes=64)
        hid_w = sb.tile([P, O], U32, name="hid_w", align_bytes=64)
        hid_s = sb.tile([P, O], U8, name="hid_s", align_bytes=64)
        woven = diff[:].rearrange("p t o -> p o t")
        nc.scalar.activation(hid_bf[:, : O // 2, :], woven[:, : O // 2, :], ACT.Abs)
        nc.vector.scalar_tensor_tensor(
            hid_bf[:, O // 2 :, :], woven[:, O // 2 :, :], -1.0, woven[:, O // 2 :, :], ALU.mult, ALU.max
        )
        nc.vector.quantize_mx(out=hid_w[:].bitcast(E5M2), scales=hid_s[:], in_=hid_bf[:].rearrange("p o t -> p (o t)"))

        p_ps = [psum.tile([P, O], F32, name=f"p_ps{h}") for h in range(PAGES)]
        p_sb = [sb.tile([P, O], F32, name=f"p_sb{h}") for h in range(PAGES)]
        for h in range(PAGES):
            nc.tensor.matmul_mx(
                out=p_ps[h][:],
                lhsT=wb_w[:, P * h : P * (h + 1)].bitcast(E5M2),
                lhsT_scale=wb_s[:, P * h : P * (h + 1)],
                rhs=hid_w[:].bitcast(E5M2),
                rhs_scale=hid_s[:],
                start=True,
                stop=True,
            )
        nc.vector.tensor_copy(p_sb[0][:], p_ps[0][:])
        nc.scalar.copy(p_sb[1][:], p_ps[1][:])
        nc.vector.tensor_copy(page[0][:].indirect(idx4[:]), p_sb[0][:])
        nc.scalar.activation(page[1][:].indirect(idx4[:]), p_sb[1][:], ACT.Copy)

        for h in range(PAGES):
            for c0 in range(0, C, CHUNK):
                y = sb.tile([P, CHUNK], F32, name=f"y{h}_{c0}")
                nc.vector.scalar_tensor_tensor(
                    y[:], old_sb[h][:, c0 : c0 + CHUNK], 0.5, page[h][:, c0 : c0 + CHUNK], ALU.mult, ALU.add
                )
                nc.sync.dma_start(out[h * P : (h + 1) * P, c0 : c0 + CHUNK], y[:])
